import numpy as np
import ml_dtypes


def mxq(x, axis, fmt="e4m3"):
    dtype, down = {"e4m3": (ml_dtypes.float8_e4m3fn, 7), "e5m2": (ml_dtypes.float8_e5m2, 14)}[fmt]
    v = np.moveaxis(np.asarray(x, np.float32).astype(ml_dtypes.bfloat16).astype(np.float64), axis, -1)
    blocks = v.reshape(v.shape[:-1] + (-1, 32))
    amax = np.abs(blocks).max(-1, keepdims=True)
    byte = np.maximum(np.where(amax > 0, np.frexp(amax)[1] - 1 + 127, 0) - down, 1)
    scale = np.exp2(byte - 127.0)
    codes = (blocks / scale).astype(np.float32).astype(dtype).astype(np.float64)
    return np.moveaxis((codes * scale).reshape(v.shape), -1, axis)


WIDE = False


def mx_kscale(k):
    if not WIDE:
        return np.ones(k)
    levels = np.array([10, -10, 5, -5, 0])
    if k % 512:
        return np.exp2(np.random.permutation(np.resize(levels, k // 32))).repeat(32)
    a = np.empty((k // 512, 16))
    for p in range(k // 512):
        a[p, :8] = np.random.permutation(np.resize(levels, 8))
        for g in range(8):
            far = levels[np.abs(levels - a[p, g]) >= 10]
            a[p, g + 8] = far[np.random.randint(len(far))]
    return np.exp2(a.ravel()).repeat(32)


BF16 = ml_dtypes.bfloat16


def bf(x):
    return np.asarray(x, np.float32).astype(BF16)


def f64(x):
    return np.asarray(x).astype(np.float64)


T, D, C, F, S = 1024, 1024, 512, 1024, 512
EPS = 1e-5


def sigmoid(z):
    return 1.0 / (1.0 + np.exp(-z))


def elu(z):
    return np.maximum(z, 0.0) + np.exp(np.minimum(z, 0.0)) - 1.0


def layer_norm(a, gain, shift):
    d = a - a.mean(axis=1, keepdims=True)
    return d / np.sqrt((d * d).mean(axis=1, keepdims=True) + EPS) * gain + shift


def draw0():
    rn = np.random.standard_normal
    s, e = mx_kscale(D), mx_kscale(C)
    t = mx_kscale(F)
    u = mx_kscale(T)
    return {"x": bf(rn((T, D)) * s),
            "k": bf(rn((T, C)) * e),
            "w_x": bf(rn((D, F)) / np.sqrt(D) / s[:, None]),
            "w_k": bf(rn((C, F)) / np.sqrt(C) / e[:, None]),
            "b_h": bf(0.3 * rn(F)),
            "v": bf((1.0 + 0.1 * rn(F)) * t),
            "r": bf(np.random.uniform(0.5, 1.5, T) * u),
            "w_f": bf(rn((F, 2 * D)) / np.sqrt(F) / t[:, None]),
            "b_f": bf(0.3 * rn(2 * D)),
            "q": bf((1.0 + 0.1 * rn(T)) / u),
            "skip": bf((1.0 + 0.1 * rn(D)) / s),
            "g_y": bf(1.0 + 0.1 * rn(D)),
            "c_y": bf(0.2 * rn(D)),
            "a_t": bf(rn((2 * S, T)) / np.sqrt(T) / u),
            "b_t": bf(0.3 * rn(2 * S)),
            "n": bf((1.0 + 0.1 * rn(F)) / t),
            "p": bf(rn((S, F))),
            "g_z": bf(1.0 + 0.1 * rn(F)),
            "c_z": bf(0.2 * rn(F))}


def core(x, k, w_x, w_k, b_h, v, r, w_f, b_f, q, skip, g_y, c_y, a_t, b_t, n, p, g_z, c_z):
    zx = mxq(f64(x), 1, "e4m3") @ mxq(f64(w_x), 0, "e4m3")
    zk = mxq(f64(k), 1, "e4m3") @ mxq(f64(w_k), 0, "e4m3")
    h = elu(zx + zk + f64(b_h)) * f64(v) * f64(r)[:, None]
    f = mxq(h, 1, "e4m3") @ mxq(f64(w_f), 0, "e4m3")
    f = f * f64(q)[:, None] + f64(b_f)
    y = layer_norm(f64(x) * f64(skip) + sigmoid(f[:, :D]) * f[:, D:], f64(g_y), f64(c_y))
    m = mxq(f64(a_t), 1, "e4m3") @ mxq(h, 0, "e4m3")
    m = m * f64(n) + f64(b_t)[:, None]
    z = layer_norm(f64(p) + sigmoid(m[:S]) * m[S:], f64(g_z), f64(c_z))
    return y, z


def e4m3fn_bytes(y):
    return np.clip(np.asarray(y, np.float64), -448.0, 448.0).astype(np.float32).astype(ml_dtypes.float8_e4m3fn).view(np.uint8)


def e4m3fn_values(b):
    return np.asarray(b, np.uint8).view(ml_dtypes.float8_e4m3fn).astype(np.float64)


def setup_inputs():
    d = draw0()
    x0 = np.asarray(d['w_f']).astype(np.float64)
    s = (np.max(np.abs(x0), axis=(1,), keepdims=True) / 448.0).astype(np.float32)
    out = {}
    for k, v in d.items():
        if k == 'w_f':
            out['w_f_bytes'] = e4m3fn_bytes(x0 / s.astype(np.float64))
            out['w_f_scale'] = s
        else:
            out[k] = v
    return out


def reference(x, k, w_x, w_k, b_h, v, r, w_f_bytes, w_f_scale, b_f, q, skip, g_y, c_y, a_t, b_t, n, p, g_z, c_z):
    return core(x, k, w_x, w_k, b_h, v, r, e4m3fn_values(w_f_bytes) * w_f_scale.astype(np.float64), b_f, q, skip, g_y, c_y, a_t, b_t, n, p, g_z, c_z)

from contextlib import ExitStack

import concourse.mybir as mybir
from concourse.masks import make_identity

T, D, C, F, S = 1024, 1024, 512, 1024, 512
EPS = 1e-5
FLOPS = 2 * T * F * (D + C) + 2 * T * F * 2 * D + 2 * 2 * S * T * F

F32 = mybir.dt.float32
BF16 = mybir.dt.bfloat16
U32 = mybir.dt.uint32
U8 = mybir.dt.uint8
F8 = mybir.dt.float8_e4m3fn
F8X4 = mybir.dt.float8_e4m3fn_x4
ACT = mybir.ActivationFunctionType
ALU = mybir.AluOpType

P = 128
H = 512


def tile_temporal_fusion_grn_f6_kernel(
    tc, x, k, w_x, w_k, b_h, v, r, w_f_bytes, w_f_scale, b_f, q, skip, g_y, c_y, a_t, b_t, n, p, g_z, c_z, y_out, z_out
):
    nc = tc.nc
    with ExitStack() as ctx:
        const = ctx.enter_context(tc.tile_pool(name="const", bufs=1))
        keep = ctx.enter_context(tc.tile_pool(name="keep", bufs=1))
        work = ctx.enter_context(tc.tile_pool(name="work", bufs=1))
        small = ctx.enter_context(tc.tile_pool(name="small", bufs=1))
        psum = ctx.enter_context(tc.psum_pool(name="psum", bufs=1))

        def unit(shape, dtype, name):
            return work.tile(shape, dtype, tag="unit", bufs=16, name=name, align_bytes=64)

        def row_tile(name):
            return work.tile([P, 1024], BF16, tag="rows", bufs=10, name=name, align_bytes=64)

        x_rows = x.rearrange("(i p) d -> i p d", p=P)
        k_pairs = k.rearrange("(b i p) d -> b p i d", i=2, p=P)
        a_rows = a_t.rearrange("(i p) d -> i p d", p=P)
        p_rows = p.rearrange("(i p) d -> i p d", p=P)
        wx_rows = w_x.rearrange("(g p j) n -> g p j n", p=P, j=4)
        wk_rows = w_k.rearrange("(p j) n -> p j n", j=4)
        wf_rows = w_f_bytes.rearrange("(g p j) n -> g p j n", p=P, j=4)

        x_raw = {}
        k_raw = {}
        a_raw = {}
        w_raw = {}
        wf_raw = {}
        p_sb = {}

        def load_x(i):
            x_raw[i] = row_tile("x_raw")
            nc.sync.dma_start(out=x_raw[i][:], in_=x_rows[i])

        def load_a(i):
            a_raw[i] = row_tile("a_raw")
            nc.sync.dma_start(out=a_raw[i][:], in_=a_rows[i])

        def load_k(i):
            k_raw[i] = work.tile([P, 2, C], BF16, tag="k_raw", bufs=2, name="k_raw", align_bytes=64)
            nc.sync.dma_start(out=k_raw[i][:], in_=k_pairs[i])

        def load_w(g, fh):
            t = unit([P, 4, H], BF16, "w_raw")
            src = wx_rows[g] if g < 2 else wk_rows
            nc.sync.dma_start(out=t[:], in_=src[:, :, fh * H : (fh + 1) * H])
            w_raw[g, fh] = t

        def load_wf(g, half):
            t = work.tile([P, 4, D], U8, tag="wf_raw", bufs=4, name="wf_raw", align_bytes=64)
            nc.sync.dma_start(out=t[:], in_=wf_rows[g][:, :, half * D : (half + 1) * D])
            wf_raw[g, half] = t

        def load_bc(vec, width, name):
            t = const.tile([P, width], BF16, tag=name, name=name, align_bytes=64)
            nc.sync.dma_start(out=t[:], in_=vec.partition_broadcast(P))
            return t

        def load_col(vec, name):
            t = const.tile([P, 2, 4], BF16, tag=name, name=name)
            nc.sync.dma_start(out=t[:], in_=vec.rearrange("(g p j) -> p g j", p=P, j=4))
            return t

        rows16 = const.tile([P, P], BF16, tag="rows16", name="rows16", align_bytes=64)
        nc.vector.memset(rows16[:], 0.0)
        ones = const.tile([P, 1], F32, tag="ones", name="ones")
        nc.vector.memset(ones[:], 1.0)
        neg_half = const.tile([P, 1], F32, tag="neg_half", name="neg_half")
        nc.vector.memset(neg_half[:], -0.5)
        ident = const.tile([P, P], F32, tag="ident", name="ident", align_bytes=64)
        make_identity(nc, ident[:])
        ident_b = const.tile([P, P], BF16, tag="ident_b", name="ident_b", align_bytes=64)
        nc.vector.tensor_copy(out=ident_b[:], in_=ident[:])

        for i in range(4):
            load_x(i)
        load_w(0, 0)
        load_w(1, 0)
        load_k(0)
        load_k(1)
        load_w(2, 0)
        b_col_b = load_col(b_h, "b_col_b")
        v_col_b = load_col(v, "v_col_b")
        r_bc = load_bc(r, T, "r_bc")
        load_w(0, 1)
        load_w(1, 1)
        load_w(2, 1)
        wfs = const.tile([P, 2, 4], F32, tag="wfs", name="wfs")
        nc.sync.dma_start(out=wfs[:], in_=w_f_scale.rearrange("(g p j) o -> p g (j o)", p=P, j=4))
        for half in range(2):
            for g in range(2):
                load_wf(g, half)
        nc.sync.dma_start(out=rows16[0:8, :], in_=q.rearrange("(i p) -> i p", p=P))
        nc.sync.dma_start(out=rows16[8:16, :], in_=b_t.rearrange("(i p) -> i p", p=P))
        skip_col = load_col(skip, "skip_col")
        bf_bc = load_bc(b_f, 2 * D, "bf_bc")
        for i in range(4, 8):
            load_x(i)
        load_k(2)
        load_k(3)
        gy_bc = load_bc(g_y, D, "gy_bc")
        cy_bc = load_bc(c_y, D, "cy_bc")
        for i in range(8):
            load_a(i)
        n_bc = load_bc(n, F, "n_bc")
        for i in range(4):
            p_sb[i] = row_tile("p_sb")
            nc.sync.dma_start(out=p_sb[i][:], in_=p_rows[i])
        gz_bc = load_bc(g_z, F, "gz_bc")
        cz_bc = load_bc(c_z, F, "cz_bc")

        b_col = const.tile([P, 8], F32, tag="b_col", name="b_col")
        nc.vector.tensor_copy(out=b_col[:], in_=b_col_b[:].rearrange("p g j -> p (g j)"))
        nv_col = const.tile([P, 8], F32, tag="nv_col", name="nv_col")
        nc.vector.tensor_scalar(
            out=nv_col[:], in0=v_col_b[:].rearrange("p g j -> p (g j)"), scalar1=-1.0, scalar2=None, op0=ALU.mult
        )

        x_i = keep.tile([P, 2, T, 4], BF16, tag="x_i", name="x_i", align_bytes=64)
        wf_c = keep.tile([P, 2, 2 * D], U32, tag="wf_c", name="wf_c", align_bytes=64)
        wf_s = keep.tile([P, 2, 2 * D], U8, tag="wf_s", name="wf_s", align_bytes=64)
        hf_c = keep.tile([P, 2, T], U32, tag="hf_c", name="hf_c", align_bytes=64)
        hf_s = keep.tile([P, 2, T], U8, tag="hf_s", name="hf_s", align_bytes=64)
        ht_c = keep.tile([P, 2, F], U32, tag="ht_c", name="ht_c", align_bytes=64)
        ht_s = keep.tile([P, 2, F], U8, tag="ht_s", name="ht_s", align_bytes=64)
        codes = {}
        k_i = {}
        a_i = {}
        hf = {}
        ht_i = {}

        def tr_bank():
            return psum.tile([P, 4, P], F32, tag="tr", bufs=2, name="tr")

        def acc_bank():
            return psum.tile([P, H], F32, tag="acc", bufs=6, name="acc")

        def word_view(t):
            return t.rearrange("p c j -> p (c j)").bitcast(F32).rearrange("p (c u) -> p c u", u=2)

        def turn_rows(src, dsts, i):
            words = src[:].bitcast(F32)
            bank = tr_bank()
            for g in range(2):
                for u in range(2):
                    nc.tensor.transpose(bank[:, 2 * g + u, :], words[:, 256 * g + u : 256 * (g + 1) : 2], ident[:])
            for g in range(2):
                nc.scalar.copy(
                    out=word_view(dsts[g])[:, (i % 4) * P : (i % 4 + 1) * P, :],
                    in_=bank[:, 2 * g : 2 * g + 2, :].rearrange("p u r -> p r u"),
                )

        def turn_x(i):
            turn_rows(x_raw[i], [x_i[:, g, (i // 4) * H : (i // 4 + 1) * H, :] for g in range(2)], i)

        def turn_a(i):
            sh = i // 4
            if i % 4 == 0:
                for g in range(2):
                    a_i[g, sh] = unit([P, H, 4], BF16, "a_i")
            turn_rows(a_raw[i], [a_i[g, sh][:] for g in range(2)], i)

        def turn_k(b):
            if b % 2 == 0:
                k_i[b // 2] = unit([P, H, 4], BF16, "k_i")
            words = k_raw[b][:].rearrange("p i d -> p (i d)").bitcast(F32)
            bank = tr_bank()
            for i in range(2):
                for u in range(2):
                    nc.tensor.transpose(bank[:, 2 * i + u, :], words[:, 256 * i + u : 256 * (i + 1) : 2], ident[:])
            dst = word_view(k_i[b // 2][:])
            nc.scalar.copy(
                out=dst[:, (b % 2) * 256 : (b % 2 + 1) * 256, :].rearrange("p (i r) u -> p i r u", i=2),
                in_=bank[:].rearrange("p (i u) r -> p i r u", i=2),
            )

        def quant(codes, scales, src):
            nc.vector.quantize_mx(out=codes.bitcast(F8X4), scales=scales, in_=src.rearrange("p c j -> p (c j)"))

        def quant_new(key, tag, bufs, src):
            ct = work.tile([P, H], U32, tag=tag + "_c", bufs=bufs, name=tag + "_c", align_bytes=64)
            st = work.tile([P, H], U8, tag=tag + "_s", bufs=bufs, name=tag + "_s", align_bytes=64)
            quant(ct[:], st[:], src)
            codes[key] = (ct, st)

        def part(key, start, width):
            ct, st = codes[key]
            return ct[:, start : start + width], st[:, start : start + width]

        def quant_x(g, th):
            src = x_i[:, g, th * H : (th + 1) * H, :] if g < 2 else k_i[th][:]
            quant_new(("x", g, th), "x", 4, src)

        w_g = {}

        def group_w(g, fh):
            t = unit([P, H, 4], BF16, "w_g")
            w_g[g, fh] = t
            dst = t[:].rearrange("p (b m) j -> p b m j", b=4)
            src = w_raw[g, fh][:].rearrange("p j (m b) -> p b m j", b=4)
            if g < 2:
                nc.vector.tensor_scalar(out=dst, in0=src, scalar1=-1.0, scalar2=None, op0=ALU.mult)
            else:
                nc.scalar.activation(out=dst, in_=src, func=ACT.Copy, scale=-1.0)

        def quant_w(g, fh):
            quant_new(("w", g, fh), "wa", 8, w_g[g, fh][:])

        def mx_group(out, passes):
            last = len(passes) - 1
            for idx, ((lc, ls), (rc, rs)) in enumerate(passes):
                nc.tensor.matmul_mx(
                    out=out,
                    lhsT=lc.bitcast(F8X4),
                    lhsT_scale=ls,
                    rhs=rc.bitcast(F8X4),
                    rhs_scale=rs,
                    start=(idx == 0),
                    stop=(idx == last),
                )

        def hidden(g, b, th):
            cols = slice(th * H, (th + 1) * H)
            if b == 0:
                hf[g, th] = work.tile([P, 4, H], BF16, tag="hf", bufs=3, name="hf", align_bytes=64)
            zp = acc_bank()
            mx_group(zp[:], [(part(("w", s, g), b * P, P), part(("x", s, th), 0, H)) for s in range(3)])
            f = 4 * g + b
            e = work.tile([P, H], F32, tag="e", bufs=4, name="e")
            nc.scalar.activation(out=e[:], in_=zp[:], func=ACT.Exp, bias=b_col[:, f : f + 1], scale=-1.0)
            nc.scalar.activation(out=e[:], in_=e[:], func=ACT.Relu, bias=ones[:, 0:1], scale=-1.0)
            nc.vector.scalar_tensor_tensor(
                out=e[:], in0=zp[:], scalar=b_col[:, f : f + 1], in1=e[:], op0=ALU.subtract, op1=ALU.min
            )
            nc.vector.scalar_tensor_tensor(
                out=hf[g, th][:, b, :], in0=e[:], scalar=nv_col[:, f : f + 1], in1=r_bc[:, cols], op0=ALU.mult, op1=ALU.mult
            )

        def quant_hf(g, th):
            cols = slice(th * H, (th + 1) * H)
            t = unit([P, H, 4], BF16, "h_g")
            nc.scalar.copy(out=t[:], in_=hf[g, th][:].rearrange("p j t -> p t j"))
            quant(hf_c[:, g, cols], hf_s[:, g, cols], t[:])

        def turn_h(g, bp, th):
            if bp == 0:
                ht_i[g, th] = unit([P, H, 4], BF16, "ht_i")
            bank = tr_bank()
            for b in range(2):
                words = hf[g, th][:, 2 * bp + b, :].bitcast(F32)
                for u in range(2):
                    nc.tensor.transpose(bank[:, 2 * b + u, :], words[:, u::2], ident[:])
            dst = word_view(ht_i[g, th][:]).rearrange("p (m b) u -> p m b u", b=4)
            nc.scalar.copy(
                out=dst[:, :, 2 * bp : 2 * bp + 2, :],
                in_=bank[:].rearrange("p (b u) m -> p m b u", b=2),
            )

        def quant_ht(th, fh):
            cols = slice(fh * H, (fh + 1) * H)
            quant(ht_c[:, th, cols], ht_s[:, th, cols], ht_i[fh, th][:])

        def quant_a(g, sh):
            quant_new(("a", g, sh), "wa", 8, a_i[g, sh][:])

        def make_wf(g, chunk):
            cols = slice(chunk * H, (chunk + 1) * H)
            wide = unit([P, 4, H], BF16, "wide")
            src = wf_raw[g, chunk // 2]
            c0 = (chunk % 2) * H
            for j in range(4):
                nc.scalar.activation(
                    out=wide[:, j, :], in_=src[:, j, c0 : c0 + H].bitcast(F8), func=ACT.Copy, scale=wfs[:, g, j : j + 1]
                )
            t = unit([P, H, 4], BF16, "wf_g")
            nc.vector.tensor_copy(out=t[:], in_=wide[:].rearrange("p j c -> p c j"))
            quant(wf_c[:, g, cols], wf_s[:, g, cols], t[:])

        def layer_norm(w, out, sums, gain, shift, dst):
            stat_v = small.tile([P, 1], F32, tag="stat_v", bufs=3, name="stat_v")
            nc.vector.tensor_scalar(
                out=stat_v[:], in0=sums[:, 0:1], scalar1=sums[:, 1:2], scalar2=-1.0 / 1024, op0=ALU.add, op1=ALU.mult
            )
            sq = work.tile([P, 1024], BF16, tag="sq", bufs=2, name="sq")
            ssq = small.tile([P, 1], F32, tag="ssq", bufs=3, name="ssq")
            nc.scalar.activation(out=sq[:], in_=w[:], func=ACT.Square, bias=stat_v[:, 0:1], accum_out=ssq[:])
            stat_g = small.tile([P, 2], F32, tag="stat_g", bufs=3, name="stat_g")
            nc.gpsimd.tensor_scalar(
                out=stat_g[:, 0:1], in0=ssq[:], scalar1=1.0 / 1024, scalar2=EPS, op0=ALU.mult, op1=ALU.add
            )
            nc.gpsimd.tensor_tensor(out=stat_g[:, 1:2], in0=stat_g[:, 0:1], in1=neg_half[:], op=ALU.pow)
            nc.vector.scalar_tensor_tensor(
                out=out[:], in0=w[:], scalar=stat_v[:, 0:1], in1=gain[:], op0=ALU.add, op1=ALU.mult
            )
            nc.vector.scalar_tensor_tensor(
                out=out[:], in0=out[:], scalar=stat_g[:, 1:2], in1=shift[:], op0=ALU.mult, op1=ALU.add
            )
            nc.sync.dma_start(out=dst, in_=out[:])

        def y_tile(i):
            rows = slice(i * P, (i + 1) * P)
            a = unit([P, 1024], F32, "a")
            w = unit([P, 1024], F32, "w")
            sums = small.tile([P, 2], F32, tag="sums", bufs=3, name="sums")
            xs = []
            for c in range(2):
                cols = slice(c * H, (c + 1) * H)
                vcols = slice(D + c * H, D + (c + 1) * H)
                pg = acc_bank()
                mx_group(pg[:], [((hf_c[:, s, rows], hf_s[:, s, rows]), (wf_c[:, s, cols], wf_s[:, s, cols])) for s in range(2)])
                nc.vector.scalar_tensor_tensor(
                    out=a[:, cols], in0=pg[:], scalar=q_col[:, i : i + 1], in1=bf_bc[:, cols], op0=ALU.mult, op1=ALU.add
                )
                pv = acc_bank()
                mx_group(pv[:], [((hf_c[:, s, rows], hf_s[:, s, rows]), (wf_c[:, s, vcols], wf_s[:, s, vcols])) for s in range(2)])
                nc.vector.scalar_tensor_tensor(
                    out=w[:, cols], in0=pv[:], scalar=q2_col[:, i : i + 1], in1=bv2_bc[:, cols], op0=ALU.mult, op1=ALU.add
                )
                px = acc_bank()
                for j in range(4):
                    nc.tensor.matmul(
                        out=px[:, j * P : (j + 1) * P],
                        lhsT=x_i[:, c, rows, j],
                        rhs=skip_diag[:, c, j, :],
                        start=True,
                        stop=True,
                    )
                xs.append(px)
            nc.scalar.activation(out=a[:], in_=a[:], func=ACT.Tanh, scale=0.5)
            nc.vector.scalar_tensor_tensor(out=w[:], in0=a[:], scalar=1.0, in1=w[:], op0=ALU.add, op1=ALU.mult)
            for c in range(2):
                cols = slice(c * H, (c + 1) * H)
                nc.vector.scalar_tensor_tensor(
                    out=w[:, cols].rearrange("p (m j) -> p m j", j=4),
                    in0=xs[c][:].rearrange("p (j m) -> p m j", j=4),
                    scalar=0.0,
                    in1=w[:, cols].rearrange("p (m j) -> p m j", j=4),
                    op0=ALU.add,
                    op1=ALU.add,
                    accum_out=sums[:, c : c + 1],
                )
            layer_norm(w, a, sums, gy_bc, cy_bc, y_out[rows, :])

        def z_tile(i):
            rows = slice(i * P, (i + 1) * P)
            a = unit([P, 1024], F32, "a")
            w = unit([P, 1024], F32, "w")
            sums = small.tile([P, 2], F32, tag="sums", bufs=3, name="sums")
            for c in range(2):
                cols = slice(c * H, (c + 1) * H)
                pg = acc_bank()
                mx_group(pg[:], [(part(("a", s, 0), i * P, P), (ht_c[:, s, cols], ht_s[:, s, cols])) for s in range(2)])
                nc.vector.tensor_tensor(out=a[:, cols], in0=pg[:], in1=n_bc[:, cols], op=ALU.mult)
                pv = acc_bank()
                mx_group(pv[:], [(part(("a", s, 1), i * P, P), (ht_c[:, s, cols], ht_s[:, s, cols])) for s in range(2)])
                nc.vector.tensor_tensor(out=w[:, cols], in0=pv[:], in1=n_bc[:, cols], op=ALU.mult)
            nc.scalar.activation(out=a[:], in_=a[:], func=ACT.Sigmoid, bias=bt_col[:, i : i + 1])
            nc.vector.scalar_tensor_tensor(
                out=w[:], in0=w[:], scalar=bt_col[:, 4 + i : 5 + i], in1=a[:], op0=ALU.add, op1=ALU.mult
            )
            nc.vector.scalar_tensor_tensor(
                out=w[:], in0=w[:], scalar=0.0, in1=p_sb[i][:], op0=ALU.add, op1=ALU.add, accum_out=sums[:, 0:1]
            )
            nc.vector.memset(sums[:, 1:2], 0.0)
            layer_norm(w, a, sums, gz_bc, cz_bc, z_out[rows, :])

        for i in range(4):
            turn_x(i)
        group_w(0, 0)
        group_w(1, 0)
        turn_k(0)
        turn_k(1)
        group_w(2, 0)
        quant_x(0, 0)
        quant_x(1, 0)
        quant_w(0, 0)
        quant_w(1, 0)
        quant_x(2, 0)
        quant_w(2, 0)
        for b in range(4):
            hidden(0, b, 0)
        for g in range(3):
            group_w(g, 1)
            quant_w(g, 1)
        for b in range(4):
            hidden(1, b, 0)
        for g in range(2):
            quant_hf(g, 0)

        cols_ps = psum.tile([P, P], BF16, tag="tr", bufs=2, name="cols_ps")
        nc.tensor.transpose(cols_ps[:], rows16[:], ident_b[:])
        qb_col = const.tile([P, 16], F32, tag="qb_col", name="qb_col")
        nc.vector.tensor_copy(out=qb_col[:], in_=cols_ps[:, 0:16])
        q_col = qb_col[:, 0:8]
        bt_col = qb_col[:, 8:16]
        q2_col = const.tile([P, 8], F32, tag="q2_col", name="q2_col")
        nc.vector.tensor_scalar(out=q2_col[:], in0=qb_col[:, 0:8], scalar1=0.5, scalar2=None, op0=ALU.mult)
        bv2_bc = const.tile([P, D], BF16, tag="bv2_bc", name="bv2_bc")
        nc.vector.tensor_scalar(out=bv2_bc[:], in0=bf_bc[:, D : 2 * D], scalar1=0.5, scalar2=None, op0=ALU.mult)
        skip_f = const.tile([P, 8], F32, tag="skip_f", name="skip_f")
        nc.vector.tensor_copy(out=skip_f[:], in_=skip_col[:].rearrange("p g j -> p (g j)"))
        skip_diag = const.tile([P, 2, 4, P], BF16, tag="skip_diag", name="skip_diag")
        for g in range(2):
            for j in range(4):
                f = 4 * g + j
                nc.gpsimd.tensor_scalar(
                    out=skip_diag[:, g, j, :], in0=ident_b[:], scalar1=skip_f[:, f : f + 1], scalar2=0.0, op0=ALU.mult, op1=ALU.add
                )

        for chunk in (0, 2, 1, 3):
            for g in range(2):
                make_wf(g, chunk)
        for g in range(2):
            for bp in range(2):
                turn_h(g, bp, 0)
            quant_ht(0, g)
        for i in range(4, 8):
            turn_x(i)
        turn_k(2)
        turn_k(3)
        for g in range(3):
            quant_x(g, 1)
        for i in range(4):
            y_tile(i)
        for g in range(2):
            for b in range(4):
                hidden(g, b, 1)
            quant_hf(g, 1)
        for g in range(2):
            for bp in range(2):
                turn_h(g, bp, 1)
            quant_ht(1, g)
        for sh in range(2):
            for i in range(4):
                turn_a(4 * sh + i)
            for g in range(2):
                quant_a(g, sh)
        for i in range(4, 8):
            y_tile(i)
        for i in range(4):
            z_tile(i)
